import numpy as np
import ml_dtypes

BF16 = ml_dtypes.bfloat16


def bf(x):
    return np.asarray(x, np.float32).astype(BF16)


def f32(x):
    return np.asarray(x, np.float32)


def f64(x):
    return np.asarray(x).astype(np.float64)


def striped(idx):
    return np.tile(idx.reshape(-1, 16).T, (8, 1))


S, A, K, M, N, E, Q = 512, 512, 256, 256, 192, 2, 96


def gelu_tanh(v):
    return 0.5 * v * (1.0 + np.tanh(np.sqrt(2.0 / np.pi) * (v + 0.044715 * v**3)))


def setup_inputs():
    return {"x": bf(np.random.standard_normal((A, S))), "wd": bf(np.random.standard_normal((A, M)) / np.sqrt(A)), "y": bf(np.random.standard_normal((K, N))), "w": bf(np.random.standard_normal((E, K, M)) / np.sqrt(K)), "b": f32(0.5 * np.random.standard_normal((M, 1))), "offs": striped(np.random.permutation(S)[:N])}


def reference(x, wd, y, w, b, offs):
    idx = offs[:16].T.reshape(-1)
    z = f64(wd).T @ f64(x)
    for e in range(E):
        z[:, idx[e * Q : (e + 1) * Q]] += f64(w)[e].T @ f64(y)[:, e * Q : (e + 1) * Q]
    return gelu_tanh(z + f64(b))

@@ -1,0 +1,68 @@
+import concourse.mybir as mybir
+
+P = 128
+A, S, M = 512, 512, 256
+E, K, N = 2, 256, 192
+Q = N // E
+DENSE_BLOCKS = A // P
+EXPERT_BLOCKS = K // P
+WINDOWS = M // P
+PIECE_COLUMNS = Q // 16
+
+BF16, F32, U16 = mybir.dt.bfloat16, mybir.dt.float32, mybir.dt.uint16
+GELU = mybir.ActivationFunctionType.Gelu_apprx_tanh
+
+FLOPS = 2 * A * M * S + 2 * K * M * N
+
+
+def tile_rows_fillproj_gelu_kernel(tc, x, wd, y, w, b, offs, out):
+    nc = tc.nc
+    with (
+        tc.tile_pool(name="held", bufs=1) as held,
+        tc.psum_pool(name="psum", bufs=1) as psum,
+    ):
+        wd_t = held.tile([P, DENSE_BLOCKS, M], BF16, name="wd_t")
+        x_t = held.tile([P, DENSE_BLOCKS, S], BF16, name="x_t")
+        w_t = held.tile([P, E, EXPERT_BLOCKS, M], BF16, name="w_t")
+        y_t = held.tile([P, EXPERT_BLOCKS, N], BF16, name="y_t")
+        b_t = held.tile([P, WINDOWS], F32, name="b_t")
+        offsets = held.tile([P, N // 16], U16, name="offsets")
+
+        x_blocks = x.rearrange("(p c) s -> p c s", p=P)
+        half = DENSE_BLOCKS // 2
+        nc.sync.dma_start(wd_t[:], wd.rearrange("(p c) m -> p c m", p=P))
+        nc.sync.dma_start(x_t[:, :half, :], x_blocks[:, :half, :])
+        nc.sync.dma_start(x_t[:, half:, :], x_blocks[:, half:, :])
+        nc.sync.dma_start(offsets[:], offs)
+        nc.sync.dma_start(y_t[:], y.rearrange("(p c) n -> p c n", p=P))
+        nc.sync.dma_start(w_t[:], w.rearrange("e (p c) m -> p e c m", p=P))
+        nc.sync.dma_start(b_t[:], b.rearrange("(a p) o -> p (a o)", p=P))
+
+        windows = [psum.tile([P, S], F32, name=f"window{m}") for m in range(WINDOWS)]
+        for c in range(DENSE_BLOCKS):
+            for m in range(WINDOWS):
+                nc.tensor.matmul(
+                    windows[m][:],
+                    wd_t[:, c, m * P : (m + 1) * P],
+                    x_t[:, c, :],
+                    start=(c == 0),
+                    stop=False,
+                )
+
+        for m in range(WINDOWS):
+            for e in range(E):
+                for c in range(EXPERT_BLOCKS):
+                    nc.tensor.matmul(
+                        windows[m][:].indirect(
+                            offsets[:, e * PIECE_COLUMNS : (e + 1) * PIECE_COLUMNS]
+                        ),
+                        w_t[:, e, c, m * P : (m + 1) * P],
+                        y_t[:, c, e * Q : (e + 1) * Q],
+                        start=False,
+                        stop=(e == E - 1 and c == EXPERT_BLOCKS - 1),
+                    )
+
+        for m in range(WINDOWS):
+            result = held.tile([P, S], F32, name=f"result{m}")
+            nc.scalar.activation(result[:], windows[m][:], GELU, bias=b_t[:, m : m + 1])
+            nc.sync.dma_start(out[m * P : (m + 1) * P, :], result[:])

@@ -8,6 +8,7 @@ DENSE_BLOCKS = A // P
 EXPERT_BLOCKS = K // P
 WINDOWS = M // P
 PIECE_COLUMNS = Q // 16
+WARM_UPS = 5
 
 BF16, F32, U16 = mybir.dt.bfloat16, mybir.dt.float32, mybir.dt.uint16
 GELU = mybir.ActivationFunctionType.Gelu_apprx_tanh
@@ -37,6 +38,14 @@ def tile_rows_fillproj_gelu_kernel(tc, x, wd, y, w, b, offs, out):
         nc.sync.dma_start(y_t[:], y.rearrange("(p c) n -> p c n", p=P))
         nc.sync.dma_start(w_t[:], w.rearrange("e (p c) m -> p e c m", p=P))
         nc.sync.dma_start(b_t[:], b.rearrange("(a p) o -> p (a o)", p=P))
+
+        zeros = held.tile([P, S], BF16, name="zeros")
+        spare = psum.tile([P, S], F32, name="spare")
+        warm = held.tile([P, 1], F32, name="warm")
+        nc.vector.memset(zeros[:], 0.0)
+        nc.scalar.activation(warm[:], zeros[:, :1], GELU)
+        for turn in range(WARM_UPS):
+            nc.tensor.matmul(spare[:], zeros[:, :P], zeros[:], start=True, stop=True)
 
         windows = [psum.tile([P, S], F32, name=f"window{m}") for m in range(WINDOWS)]
         for c in range(DENSE_BLOCKS):

@@ -8,7 +8,7 @@ DENSE_BLOCKS = A // P
 EXPERT_BLOCKS = K // P
 WINDOWS = M // P
 PIECE_COLUMNS = Q // 16
-WARM_UPS = 5
+WARM_UPS = 16
 
 BF16, F32, U16 = mybir.dt.bfloat16, mybir.dt.float32, mybir.dt.uint16
 GELU = mybir.ActivationFunctionType.Gelu_apprx_tanh
@@ -29,23 +29,24 @@ def tile_rows_fillproj_gelu_kernel(tc, x, wd, y, w, b, offs, out):
         b_t = held.tile([P, WINDOWS], F32, name="b_t")
         offsets = held.tile([P, N // 16], U16, name="offsets")
 
+        wd_blocks = wd.rearrange("(p c) m -> p c m", p=P)
         x_blocks = x.rearrange("(p c) s -> p c s", p=P)
         half = DENSE_BLOCKS // 2
-        nc.sync.dma_start(wd_t[:], wd.rearrange("(p c) m -> p c m", p=P))
-        nc.sync.dma_start(x_t[:, :half, :], x_blocks[:, :half, :])
-        nc.sync.dma_start(x_t[:, half:, :], x_blocks[:, half:, :])
+        for blocks in (slice(0, half), slice(half, DENSE_BLOCKS)):
+            nc.sync.dma_start(wd_t[:, blocks, :], wd_blocks[:, blocks, :])
+            nc.sync.dma_start(x_t[:, blocks, :], x_blocks[:, blocks, :])
         nc.sync.dma_start(offsets[:], offs)
         nc.sync.dma_start(y_t[:], y.rearrange("(p c) n -> p c n", p=P))
         nc.sync.dma_start(w_t[:], w.rearrange("e (p c) m -> p e c m", p=P))
         nc.sync.dma_start(b_t[:], b.rearrange("(a p) o -> p (a o)", p=P))
 
-        zeros = held.tile([P, S], BF16, name="zeros")
-        spare = psum.tile([P, S], F32, name="spare")
+        zeros = held.tile([P, P], BF16, name="zeros")
+        spare = psum.tile([P, P], F32, name="spare")
         warm = held.tile([P, 1], F32, name="warm")
         nc.vector.memset(zeros[:], 0.0)
         nc.scalar.activation(warm[:], zeros[:, :1], GELU)
         for turn in range(WARM_UPS):
-            nc.tensor.matmul(spare[:], zeros[:, :P], zeros[:], start=True, stop=True)
+            nc.tensor.matmul(spare[:], zeros[:], zeros[:], start=True, stop=True)
 
         windows = [psum.tile([P, S], F32, name=f"window{m}") for m in range(WINDOWS)]
         for c in range(DENSE_BLOCKS):

@@ -74,5 +74,10 @@ def tile_rows_fillproj_gelu_kernel(tc, x, wd, y, w, b, offs, out):
 
         for m in range(WINDOWS):
             result = held.tile([P, S], F32, name=f"result{m}")
-            nc.scalar.activation(result[:], windows[m][:], GELU, bias=b_t[:, m : m + 1])
-            nc.sync.dma_start(out[m * P : (m + 1) * P, :], result[:])
+            parts = 2 if m == WINDOWS - 1 else 1
+            for part in range(parts):
+                columns = slice(part * S // parts, (part + 1) * S // parts)
+                nc.scalar.activation(
+                    result[:, columns], windows[m][:, columns], GELU, bias=b_t[:, m : m + 1]
+                )
+                nc.sync.dma_start(out[m * P : (m + 1) * P, columns], result[:, columns])

import concourse.mybir as mybir

P = 128
A, S, M = 512, 512, 256
E, K, N = 2, 256, 192
Q = N // E
DENSE_BLOCKS = A // P
EXPERT_BLOCKS = K // P
WINDOWS = M // P
PIECE_COLUMNS = Q // 16
WARM_UPS = 16

BF16, F32, U16 = mybir.dt.bfloat16, mybir.dt.float32, mybir.dt.uint16
GELU = mybir.ActivationFunctionType.Gelu_apprx_tanh

FLOPS = 2 * A * M * S + 2 * K * M * N


def tile_rows_fillproj_gelu_kernel(tc, x, wd, y, w, b, offs, out):
    nc = tc.nc
    with (
        tc.tile_pool(name="held", bufs=1) as held,
        tc.psum_pool(name="psum", bufs=1) as psum,
    ):
        wd_t = held.tile([P, DENSE_BLOCKS, M], BF16, name="wd_t")
        x_t = held.tile([P, DENSE_BLOCKS, S], BF16, name="x_t")
        w_t = held.tile([P, E, EXPERT_BLOCKS, M], BF16, name="w_t")
        y_t = held.tile([P, EXPERT_BLOCKS, N], BF16, name="y_t")
        b_t = held.tile([P, WINDOWS], F32, name="b_t")
        offsets = held.tile([P, N // 16], U16, name="offsets")

        wd_blocks = wd.rearrange("(p c) m -> p c m", p=P)
        x_blocks = x.rearrange("(p c) s -> p c s", p=P)
        half = DENSE_BLOCKS // 2
        for blocks in (slice(0, half), slice(half, DENSE_BLOCKS)):
            nc.sync.dma_start(wd_t[:, blocks, :], wd_blocks[:, blocks, :])
            nc.sync.dma_start(x_t[:, blocks, :], x_blocks[:, blocks, :])
        nc.sync.dma_start(offsets[:], offs)
        nc.sync.dma_start(y_t[:], y.rearrange("(p c) n -> p c n", p=P))
        nc.sync.dma_start(w_t[:], w.rearrange("e (p c) m -> p e c m", p=P))
        nc.sync.dma_start(b_t[:], b.rearrange("(a p) o -> p (a o)", p=P))

        zeros = held.tile([P, P], BF16, name="zeros")
        spare = psum.tile([P, P], F32, name="spare")
        warm = held.tile([P, 1], F32, name="warm")
        nc.vector.memset(zeros[:], 0.0)
        nc.scalar.activation(warm[:], zeros[:, :1], GELU)
        for turn in range(WARM_UPS):
            nc.tensor.matmul(spare[:], zeros[:], zeros[:], start=True, stop=True)

        windows = [psum.tile([P, S], F32, name=f"window{m}") for m in range(WINDOWS)]
        for c in range(DENSE_BLOCKS):
            for m in range(WINDOWS):
                nc.tensor.matmul(
                    windows[m][:],
                    wd_t[:, c, m * P : (m + 1) * P],
                    x_t[:, c, :],
                    start=(c == 0),
                    stop=False,
                )

        for m in range(WINDOWS):
            for e in range(E):
                for c in range(EXPERT_BLOCKS):
                    nc.tensor.matmul(
                        windows[m][:].indirect(
                            offsets[:, e * PIECE_COLUMNS : (e + 1) * PIECE_COLUMNS]
                        ),
                        w_t[:, e, c, m * P : (m + 1) * P],
                        y_t[:, c, e * Q : (e + 1) * Q],
                        start=False,
                        stop=(e == E - 1 and c == EXPERT_BLOCKS - 1),
                    )

        for m in range(WINDOWS):
            result = held.tile([P, S], F32, name=f"result{m}")
            parts = 2 if m == WINDOWS - 1 else 1
            for part in range(parts):
                columns = slice(part * S // parts, (part + 1) * S // parts)
                nc.scalar.activation(
                    result[:, columns], windows[m][:, columns], GELU, bias=b_t[:, m : m + 1]
                )
                nc.sync.dma_start(out[m * P : (m + 1) * P, columns], result[:, columns])
